import numpy as np
import ml_dtypes


def mxq(x, axis, fmt="e4m3"):
    dtype, down = {"e4m3": (ml_dtypes.float8_e4m3fn, 7), "e5m2": (ml_dtypes.float8_e5m2, 14)}[fmt]
    v = np.moveaxis(np.asarray(x, np.float32).astype(ml_dtypes.bfloat16).astype(np.float64), axis, -1)
    blocks = v.reshape(v.shape[:-1] + (-1, 32))
    amax = np.abs(blocks).max(-1, keepdims=True)
    byte = np.maximum(np.where(amax > 0, np.frexp(amax)[1] - 1 + 127, 0) - down, 1)
    scale = np.exp2(byte - 127.0)
    codes = (blocks / scale).astype(np.float32).astype(dtype).astype(np.float64)
    return np.moveaxis((codes * scale).reshape(v.shape), -1, axis)


WIDE = False


def mx_kscale(k):
    if not WIDE:
        return np.ones(k)
    levels = np.array([10, -10, 5, -5, 0])
    if k % 512:
        return np.exp2(np.random.permutation(np.resize(levels, k // 32))).repeat(32)
    a = np.empty((k // 512, 16))
    for p in range(k // 512):
        a[p, :8] = np.random.permutation(np.resize(levels, 8))
        for g in range(8):
            far = levels[np.abs(levels - a[p, g]) >= 10]
            a[p, g + 8] = far[np.random.randint(len(far))]
    return np.exp2(a.ravel()).repeat(32)


BF16 = ml_dtypes.bfloat16


def bf(x):
    return np.asarray(x, np.float32).astype(BF16)


def f64(x):
    return np.asarray(x).astype(np.float64)


E2M1 = np.array([0.0, 0.5, 1.0, 1.5, 2.0, 3.0, 4.0, 6.0, -0.0, -0.5, -1.0, -1.5, -2.0, -3.0, -4.0, -6.0])


def pack_weight(w, fmt):
    k, n = w.shape
    w = f64(bf(w)).reshape(k // 32, 32, n)
    amax = np.abs(w).max(1)
    if fmt == "e4m3":
        byte = np.frexp(amax)[1] - 1 + 127 - 7
    else:
        mant, ex = np.frexp(amax / 6.0)
        byte = np.where(mant > 0.5, ex, ex - 1) + 127
    byte = np.clip(np.where(amax > 0, byte, 1), 1, 254)
    scaled = (w * np.exp2(127.0 - byte)[:, None, :]).reshape(k, n).astype(np.float32)
    by_word = np.ascontiguousarray(scaled.reshape(k // 512, 128, 4, n).transpose(0, 1, 3, 2))
    if fmt == "e4m3":
        words = by_word.astype(ml_dtypes.float8_e4m3fn).view(np.uint8)
    else:
        c = by_word.astype(ml_dtypes.float4_e2m1fn).view(np.uint8) & 0xF
        words = c[..., 0::2] | (c[..., 1::2] << 4)
    return np.ascontiguousarray(words), np.ascontiguousarray(byte.astype(np.uint8).reshape(k // 512, 16, n))


def unpack_weight(words, scales, fmt):
    g, p, n, _ = words.shape
    if fmt == "e4m3":
        vals = np.ascontiguousarray(words).view(ml_dtypes.float8_e4m3fn).astype(np.float64)
    else:
        nib = np.empty((g, p, n, 4), np.uint8)
        nib[..., 0::2] = words & 0xF
        nib[..., 1::2] = words >> 4
        vals = E2M1[nib]
    vals = vals * np.repeat(np.exp2(scales.astype(np.float64) - 127.0), 8, axis=1)[..., None]
    return vals.transpose(0, 1, 3, 2).reshape(g * 512, n)
def pack4(w):
    words, scales = pack_weight(w, "e2m1")
    return words.reshape(words.shape[0], 128, -1), scales


def unpack4(words, scales):
    return unpack_weight(words.reshape(words.shape[0], 128, -1, 2), scales, "e2m1")


E4M3FN = np.array([(-1.0 if i & 128 else 1.0) * ((1.0 + (i & 7) / 8.0) * 2.0 ** (((i >> 3) & 15) - 7) if i & 120 else (i & 7) * 2.0 ** -9) for i in range(256)])


def e4m3fn_bytes(y):
    return np.clip(np.asarray(y, np.float64), -448.0, 448.0).astype(np.float32).astype(ml_dtypes.float8_e4m3fn).view(np.uint8)


def e4m3fn_values(b):
    return E4M3FN[b]


M, K, J, N, B = 1024, 2048, 1024, 1536, 128


def setup_inputs():
    s, t = mx_kscale(K), mx_kscale(J)
    x = np.random.standard_normal((M, K)) * s
    scale = (np.abs(x).reshape(M, K // B, B).max(axis=2) / 448.0).astype(np.float32)
    tbank = np.random.standard_normal((K, N)) / np.sqrt(K) / s[:, None]
    words, scales = pack4(tbank)
    return {"teacher_bytes": e4m3fn_bytes(x / np.repeat(f64(scale), B, axis=1)),
            "teacher_scale": scale,
            "tbank_words": words,
            "tbank_scales": scales,
            "student": bf(np.random.standard_normal((M, J)) * t),
            "sbank": bf(np.random.standard_normal((N, J)) / np.sqrt(J) / t),
            "trust": bf(np.random.uniform(0.5, 1.5, N))}


def reference(teacher_bytes, teacher_scale, tbank_words, tbank_scales, student, sbank, trust):
    teacher = e4m3fn_values(teacher_bytes) * np.repeat(f64(teacher_scale), B, axis=1)
    rel_t = mxq(teacher, 1, "e4m3") @ unpack4(tbank_words, tbank_scales)
    rel_s = mxq(f64(student), 1, "e4m3") @ mxq(f64(sbank), 1, "e4m3").T
    gap = rel_t - rel_s
    pair_loss = np.square(gap) * f64(trust)
    sample_loss = pair_loss.mean(axis=1)
    return pair_loss, sample_loss

@@ -1,0 +1,323 @@
+from contextlib import ExitStack
+
+import concourse.mybir as mybir
+from concourse.masks import make_identity
+
+M, K, J, N = 1024, 2048, 1024, 1536
+FLOPS = 2 * M * N * (K + J)
+
+F32 = mybir.dt.float32
+BF16 = mybir.dt.bfloat16
+I32 = mybir.dt.int32
+U32 = mybir.dt.uint32
+U8 = mybir.dt.uint8
+FP8 = mybir.dt.float8_e4m3fn
+FP8X4 = mybir.dt.float8_e4m3fn_x4
+FP4X4 = mybir.dt.float4_e2m1fn_x4
+MULT = mybir.AluOpType.mult
+SQUARE = mybir.ActivationFunctionType.Square
+
+P = 128
+TILES = M // P
+CHUNK = 512
+CHUNKS = N // CHUNK
+GT = K // 512
+GS = J // 512
+
+
+def tile_bank_relation_distill_d6_kernel(
+    tc, teacher_bytes, teacher_scale, tbank_words, tbank_scales, student, sbank, trust, out_0, out_1
+):
+    nc = tc.nc
+    with ExitStack() as ctx:
+        const = ctx.enter_context(tc.tile_pool(name="const", bufs=1))
+        work = ctx.enter_context(tc.tile_pool(name="work", bufs=3))
+        turned = ctx.enter_context(tc.psum_pool(name="turned", bufs=4))
+        sums_pool = ctx.enter_context(tc.psum_pool(name="acc", bufs=4))
+
+        ident = const.tile([P, P], F32, name="ident")
+        make_identity(nc, ident[:])
+        ones = const.tile([P, P], BF16, name="ones")
+        trust_row = const.tile([P, N], BF16, name="trust_row")
+        nc.gpsimd.memset(trust_row[:], 0.0)
+        nc.gpsimd.memset(ones[:], 1.0)
+        trust_all = const.tile([P, N], F32, name="trust_all")
+        tb_words = const.tile([P, GT, 2 * N], U8, name="tb_words", align_bytes=64)
+        tb_scales = const.tile([P, GT, N], U8, name="tb_scales", align_bytes=64)
+        nc.vector.memset(tb_scales[:].rearrange("p g n -> p (g n)").bitcast(I32), 0)
+        scale = const.tile([P, TILES, K // P], F32, name="scale")
+        neg = const.tile([P, TILES, K // P], F32, name="neg")
+        parts = const.tile([P, TILES, CHUNKS], F32, name="parts")
+        means = const.tile([P, TILES], F32, name="means")
+
+        t_view = teacher_bytes.rearrange("(p m) k -> p m k", m=TILES)
+        s_view = student.rearrange("(p m) k -> p m k", m=TILES)
+        o_view = out_0.rearrange("(p m) n -> p m n", m=TILES)
+
+        t_raw = [const.tile([P, K], U8, name="t_raw%d" % m, align_bytes=64) for m in range(TILES)]
+        s_raw = [const.tile([P, J], BF16, name="s_raw%d" % m, align_bytes=64) for m in range(TILES)]
+        b_raw = [const.tile([P, J], BF16, name="b_raw%d" % i, align_bytes=64) for i in range(N // P)]
+        b_codes = const.tile([P, CHUNKS, GS, CHUNK], U32, name="b_codes", align_bytes=64)
+        b_scales = const.tile([P, CHUNKS, GS, CHUNK], U8, name="b_scales", align_bytes=64)
+
+        def load_s(m):
+            nc.sync.dma_start(out=s_raw[m][:], in_=s_view[:, m, :])
+
+        def load_t(m):
+            nc.sync.dma_start(out=t_raw[m][:], in_=t_view[:, m, :])
+
+        def load_b(c):
+            for i in range(4 * c, 4 * c + 4):
+                nc.sync.dma_start(out=b_raw[i][:], in_=sbank[P * i : P * (i + 1), :])
+
+        def load_words(c):
+            cols = slice(2 * CHUNK * c, 2 * CHUNK * (c + 1))
+            nc.sync.dma_start(
+                out=tb_words[:, :, cols].bitcast(I32),
+                in_=tbank_words[:, :, cols].rearrange("g p w -> p g w").bitcast(I32),
+            )
+
+        live = {}
+
+        def perm_s(m):
+            xs = work.tile([P, GS, 2, P], F32, name="xs")
+            live["xs", m] = xs
+            nc.vector.tensor_copy(
+                out=xs[:], in_=s_raw[m][:].bitcast(F32).rearrange("p (g w u) -> p g u w", g=GS, u=2)
+            )
+
+        def turn_s(m):
+            bank = turned.tile([P, GS, 2, P], F32, name="bank")
+            live["bs", m] = bank
+            for g in range(GS):
+                for u in range(2):
+                    nc.tensor.transpose(bank[:, g, u, :], live["xs", m][:, g, u, :], ident[:])
+
+        def take_s(m):
+            grouped = work.tile([P, GS, P, 2], F32, name="s_grouped", align_bytes=64)
+            live["gs", m] = grouped
+            nc.scalar.copy(out=grouped[:], in_=live["bs", m][:].rearrange("p g u r -> p g r u"))
+
+        def quant_s(m):
+            codes = work.tile([P, GS, P], U32, name="s_codes", align_bytes=64)
+            scales = work.tile([P, GS, P], U8, name="s_scales", align_bytes=64)
+            live["cs", m] = (codes, scales)
+            nc.vector.quantize_mx(
+                out=codes[:].rearrange("p g r -> p (g r)").bitcast(FP8X4),
+                scales=scales[:].rearrange("p g r -> p (g r)"),
+                in_=live["gs", m][:].rearrange("p g r u -> p (g r u)").bitcast(BF16),
+            )
+
+        def widen(m, lo, hi):
+            if lo == 0:
+                live["xt", m] = work.tile([P, GT, 2, P, 2], BF16, name="xt", align_bytes=64)
+            xt = live["xt", m]
+            for c in range(lo, hi):
+                g, q = divmod(c, 4)
+                nc.vector.tensor_scalar(
+                    out=xt[:, g, :, 32 * q : 32 * (q + 1), :].rearrange("p u w e -> p w u e"),
+                    in0=t_raw[m][:, P * c : P * (c + 1)].bitcast(FP8).rearrange("p (w u e) -> p w u e", u=2, e=2),
+                    scalar1=neg[:, m, c : c + 1],
+                    scalar2=None,
+                    op0=MULT,
+                )
+
+        def turn_t(m):
+            words = live["xt", m][:].rearrange("p g u w e -> p (g u w e)").bitcast(F32)
+            for h in range(2):
+                bank = turned.tile([P, 2, 2, P], F32, name="bank")
+                live["bt", m, h] = bank
+                for g in range(2):
+                    for u in range(2):
+                        at = P * (2 * (2 * h + g) + u)
+                        nc.tensor.transpose(bank[:, g, u, :], words[:, at : at + P], ident[:])
+
+        def take_t(m):
+            grouped = work.tile([P, GT, P, 2], F32, name="t_grouped", align_bytes=64)
+            live["gt", m] = grouped
+            for h in range(2):
+                nc.scalar.copy(
+                    out=grouped[:, 2 * h : 2 * h + 2], in_=live["bt", m, h][:].rearrange("p g u r -> p g r u")
+                )
+
+        def quant_t(m):
+            codes = work.tile([P, GT, P], U32, name="t_codes", align_bytes=64)
+            scales = work.tile([P, GT, P], U8, name="t_scales", align_bytes=64)
+            live["ct", m] = (codes, scales)
+            nc.vector.quantize_mx(
+                out=codes[:].rearrange("p g r -> p (g r)").bitcast(FP8X4),
+                scales=scales[:].rearrange("p g r -> p (g r)"),
+                in_=live["gt", m][:].rearrange("p g r u -> p (g r u)").bitcast(BF16),
+            )
+
+        def turn_b(i):
+            bank = turned.tile([P, GS, 2, P], F32, name="bank")
+            live["bb", i] = bank
+            words = b_raw[i][:].bitcast(F32)
+            for g in range(GS):
+                for u in range(2):
+                    nc.tensor.transpose(bank[:, g, u, :], words[:, 256 * g + u : 256 * (g + 1) : 2], ident[:])
+
+        def take_b(i, on_scalar):
+            c, j = divmod(i, 4)
+            if j == 0:
+                live["gb", c] = work.tile([P, GS, CHUNK, 2], F32, name="b_grouped", align_bytes=64)
+            dst = live["gb", c][:, :, P * j : P * (j + 1), :]
+            src = live["bb", i][:].rearrange("p g u r -> p g r u")
+            if on_scalar:
+                nc.scalar.copy(out=dst, in_=src)
+            else:
+                nc.vector.tensor_copy(out=dst, in_=src)
+
+        def quant_b(c):
+            for g in range(GS):
+                nc.vector.quantize_mx(
+                    out=b_codes[:, c, g, :].bitcast(FP8X4),
+                    scales=b_scales[:, c, g, :],
+                    in_=live["gb", c][:, g].rearrange("p r u -> p (r u)").bitcast(BF16),
+                )
+
+        def mm_s(m, n):
+            acc = sums_pool.tile([P, CHUNK], F32, name="acc")
+            live["acc", m, n] = acc
+            codes, scales = live["cs", m]
+            for g in range(GS):
+                nc.tensor.matmul_mx(
+                    out=acc[:],
+                    lhsT=codes[:, g, :].bitcast(FP8X4),
+                    lhsT_scale=scales[:, g, :],
+                    rhs=b_codes[:, n, g, :].bitcast(FP8X4),
+                    rhs_scale=b_scales[:, n, g, :],
+                    start=(g == 0),
+                    stop=False,
+                )
+
+        def mm_t(m, n):
+            acc = live["acc", m, n]
+            codes, scales = live["ct", m]
+            for g in range(GT):
+                nc.tensor.matmul_mx(
+                    out=acc[:],
+                    lhsT=codes[:, g, :].bitcast(FP8X4),
+                    lhsT_scale=scales[:, g, :],
+                    rhs=tb_words[:, g, 2 * CHUNK * n : 2 * CHUNK * (n + 1)].bitcast(FP4X4),
+                    rhs_scale=tb_scales[:, g, CHUNK * n : CHUNK * (n + 1)],
+                    start=False,
+                    stop=(g == GT - 1),
+                )
+
+        def square(m, n):
+            sq = work.tile([P, CHUNK], F32, name="sq")
+            live["sq", m, n] = sq
+            nc.scalar.activation(out=sq[:], in_=live["acc", m, n][:], func=SQUARE)
+
+        def weigh(m, n):
+            res = work.tile([P, CHUNK], F32, name="res")
+            cols = slice(CHUNK * n, CHUNK * (n + 1))
+            nc.vector.scalar_tensor_tensor(
+                out=res[:],
+                in0=live["sq", m, n][:],
+                scalar=1.0,
+                in1=trust_all[:, cols],
+                op0=MULT,
+                op1=MULT,
+                accum_out=parts[:, m, n : n + 1],
+            )
+            nc.sync.dma_start(out=o_view[:, m, cols], in_=res[:])
+
+        with tc.manual_schedule():
+            nc.sync.dma_start(out=scale[:], in_=teacher_scale.rearrange("(p m) c -> p m c", m=TILES))
+            load_s(0)
+            load_b(0)
+            load_t(0)
+            load_b(1)
+            for q in range(4):
+                nc.sync.dma_start(
+                    out=tb_scales[32 * q : 32 * q + 4, :, :].bitcast(I32),
+                    in_=tbank_scales[:, 4 * q : 4 * q + 4, :].rearrange("g q n -> q g n").bitcast(I32),
+                )
+            load_words(0)
+            nc.sync.dma_start(out=trust_row[0:1, :], in_=trust.rearrange("(o n) -> o n", o=1))
+            load_b(2)
+            load_words(1)
+            load_words(2)
+            for m in range(1, TILES):
+                load_t(m)
+                load_s(m)
+
+            nc.vector.tensor_scalar(out=neg[:], in0=scale[:], scalar1=-1.0, scalar2=None, op0=MULT)
+            perm_s(0)
+            turn_s(0)
+            take_s(0)
+            for i in range(4):
+                turn_b(i)
+                take_b(i, i % 2 == 0)
+                if i == 1:
+                    quant_s(0)
+            widen(0, 0, 16)
+            quant_b(0)
+            turn_t(0)
+            take_t(0)
+            for i in range(4, 8):
+                turn_b(i)
+                take_b(i, i % 2 == 0)
+                if i == 5:
+                    quant_t(0)
+            mm_s(0, 0)
+            quant_b(1)
+            for i in range(8, 12):
+                turn_b(i)
+                take_b(i, i % 2 == 0)
+            mm_s(0, 1)
+            mm_t(0, 0)
+            quant_b(2)
+            for n in range(CHUNKS):
+                bank = turned.tile([P, CHUNK], F32, name="bank")
+                cols = slice(CHUNK * n, CHUNK * (n + 1))
+                nc.tensor.matmul(bank[:], ones[:], trust_row[:, cols], start=True, stop=True)
+                nc.scalar.copy(out=trust_all[:, cols], in_=bank[:])
+            perm_s(1)
+            widen(1, 0, 16)
+            square(0, 0)
+            weigh(0, 0)
+            mm_s(0, 2)
+            mm_t(0, 1)
+            square(0, 1)
+            weigh(0, 1)
+            turn_s(1)
+            turn_t(1)
+            take_s(1)
+            take_t(1)
+            perm_s(2)
+            quant_s(1)
+            quant_t(1)
+            mm_t(0, 2)
+            square(0, 2)
+            weigh(0, 2)
+            widen(2, 0, 16)
+
+            for m in range(1, TILES):
+                ahead = m + 1 < TILES
+                further = m + 2 < TILES
+                if ahead:
+                    turn_s(m + 1)
+                    turn_t(m + 1)
+                    take_s(m + 1)
+                    take_t(m + 1)
+                if further:
+                    perm_s(m + 2)
+                if ahead:
+                    quant_s(m + 1)
+                    quant_t(m + 1)
+                for n in range(CHUNKS):
+                    mm_s(m, n)
+                    mm_t(m, n)
+                    square(m, n)
+                    if further and n < 2:
+                        widen(m + 2, 8 * n, 8 * n + 8)
+                    weigh(m, n)
+
+            total = const.tile([P, TILES], F32, name="total")
+            nc.vector.reduce_sum(out=total[:], in_=parts[:], axis=mybir.AxisListType.X)
+            nc.vector.tensor_scalar(out=means[:], in0=total[:], scalar1=1.0 / N, scalar2=None, op0=MULT)
+            nc.sync.dma_start(out=out_1.rearrange("(p m) -> p m", m=TILES), in_=means[:])

@@ -32,15 +32,19 @@ def tile_bank_relation_distill_d6_kernel(
     with ExitStack() as ctx:
         const = ctx.enter_context(tc.tile_pool(name="const", bufs=1))
         work = ctx.enter_context(tc.tile_pool(name="work", bufs=3))
+        keep = ctx.enter_context(tc.tile_pool(name="keep", bufs=6))
+        outs = ctx.enter_context(tc.tile_pool(name="outs", bufs=6))
         turned = ctx.enter_context(tc.psum_pool(name="turned", bufs=4))
         sums_pool = ctx.enter_context(tc.psum_pool(name="acc", bufs=4))
 
-        ident = const.tile([P, P], F32, name="ident")
-        make_identity(nc, ident[:])
+        warm = const.tile([P, CHUNK], BF16, name="warm")
+        nc.gpsimd.memset(warm[:].bitcast(I32), 0)
         ones = const.tile([P, P], BF16, name="ones")
         trust_row = const.tile([P, N], BF16, name="trust_row")
-        nc.gpsimd.memset(trust_row[:], 0.0)
+        nc.vector.memset(trust_row[:].bitcast(I32), 0)
         nc.gpsimd.memset(ones[:], 1.0)
+        ident = const.tile([P, P], F32, name="ident")
+        make_identity(nc, ident[:])
         trust_all = const.tile([P, N], F32, name="trust_all")
         tb_words = const.tile([P, GT, 2 * N], U8, name="tb_words", align_bytes=64)
         tb_scales = const.tile([P, GT, N], U8, name="tb_scales", align_bytes=64)
@@ -89,9 +93,14 @@ def tile_bank_relation_distill_d6_kernel(
         def turn_s(m):
             bank = turned.tile([P, GS, 2, P], F32, name="bank")
             live["bs", m] = bank
+            words = s_raw[m][:].bitcast(F32)
             for g in range(GS):
                 for u in range(2):
-                    nc.tensor.transpose(bank[:, g, u, :], live["xs", m][:, g, u, :], ident[:])
+                    if ("xs", m) in live:
+                        rows = live["xs", m][:, g, u, :]
+                    else:
+                        rows = words[:, 256 * g + u : 256 * (g + 1) : 2]
+                    nc.tensor.transpose(bank[:, g, u, :], rows, ident[:])
 
         def take_s(m):
             grouped = work.tile([P, GS, P, 2], F32, name="s_grouped", align_bytes=64)
@@ -99,8 +108,8 @@ def tile_bank_relation_distill_d6_kernel(
             nc.scalar.copy(out=grouped[:], in_=live["bs", m][:].rearrange("p g u r -> p g r u"))
 
         def quant_s(m):
-            codes = work.tile([P, GS, P], U32, name="s_codes", align_bytes=64)
-            scales = work.tile([P, GS, P], U8, name="s_scales", align_bytes=64)
+            codes = keep.tile([P, GS, P], U32, name="s_codes", align_bytes=64)
+            scales = keep.tile([P, GS, P], U8, name="s_scales", align_bytes=64)
             live["cs", m] = (codes, scales)
             nc.vector.quantize_mx(
                 out=codes[:].rearrange("p g r -> p (g r)").bitcast(FP8X4),
@@ -132,17 +141,19 @@ def tile_bank_relation_distill_d6_kernel(
                         at = P * (2 * (2 * h + g) + u)
                         nc.tensor.transpose(bank[:, g, u, :], words[:, at : at + P], ident[:])
 
-        def take_t(m):
-            grouped = work.tile([P, GT, P, 2], F32, name="t_grouped", align_bytes=64)
-            live["gt", m] = grouped
-            for h in range(2):
-                nc.scalar.copy(
-                    out=grouped[:, 2 * h : 2 * h + 2], in_=live["bt", m, h][:].rearrange("p g u r -> p g r u")
-                )
+        def take_t(m, h, on_scalar=True):
+            if h == 0:
+                live["gt", m] = work.tile([P, GT, P, 2], F32, name="t_grouped", align_bytes=64)
+            dst = live["gt", m][:, 2 * h : 2 * h + 2]
+            src = live["bt", m, h][:].rearrange("p g u r -> p g r u")
+            if on_scalar:
+                nc.scalar.copy(out=dst, in_=src)
+            else:
+                nc.vector.tensor_copy(out=dst, in_=src)
 
         def quant_t(m):
-            codes = work.tile([P, GT, P], U32, name="t_codes", align_bytes=64)
-            scales = work.tile([P, GT, P], U8, name="t_scales", align_bytes=64)
+            codes = keep.tile([P, GT, P], U32, name="t_codes", align_bytes=64)
+            scales = keep.tile([P, GT, P], U8, name="t_scales", align_bytes=64)
             live["ct", m] = (codes, scales)
             nc.vector.quantize_mx(
                 out=codes[:].rearrange("p g r -> p (g r)").bitcast(FP8X4),
@@ -177,147 +188,263 @@ def tile_bank_relation_distill_d6_kernel(
                     in_=live["gb", c][:, g].rearrange("p r u -> p (r u)").bitcast(BF16),
                 )
 
-        def mm_s(m, n):
-            acc = sums_pool.tile([P, CHUNK], F32, name="acc")
-            live["acc", m, n] = acc
+        def passes_s(m, n, acc, lo, hi, first, last):
             codes, scales = live["cs", m]
             for g in range(GS):
                 nc.tensor.matmul_mx(
-                    out=acc[:],
+                    out=acc,
                     lhsT=codes[:, g, :].bitcast(FP8X4),
                     lhsT_scale=scales[:, g, :],
-                    rhs=b_codes[:, n, g, :].bitcast(FP8X4),
-                    rhs_scale=b_scales[:, n, g, :],
-                    start=(g == 0),
-                    stop=False,
+                    rhs=b_codes[:, n, g, lo:hi].bitcast(FP8X4),
+                    rhs_scale=b_scales[:, n, g, lo:hi],
+                    start=first and g == 0,
+                    stop=last and g == GS - 1,
                 )
 
-        def mm_t(m, n):
-            acc = live["acc", m, n]
+        def passes_t(m, n, acc, lo, hi, first, last):
             codes, scales = live["ct", m]
             for g in range(GT):
                 nc.tensor.matmul_mx(
-                    out=acc[:],
+                    out=acc,
                     lhsT=codes[:, g, :].bitcast(FP8X4),
                     lhsT_scale=scales[:, g, :],
-                    rhs=tb_words[:, g, 2 * CHUNK * n : 2 * CHUNK * (n + 1)].bitcast(FP4X4),
-                    rhs_scale=tb_scales[:, g, CHUNK * n : CHUNK * (n + 1)],
-                    start=False,
-                    stop=(g == GT - 1),
+                    rhs=tb_words[:, g, 2 * (CHUNK * n + lo) : 2 * (CHUNK * n + hi)].bitcast(FP4X4),
+                    rhs_scale=tb_scales[:, g, CHUNK * n + lo : CHUNK * n + hi],
+                    start=first and g == 0,
+                    stop=last and g == GT - 1,
                 )
 
-        def square(m, n):
-            sq = work.tile([P, CHUNK], F32, name="sq")
-            live["sq", m, n] = sq
-            nc.scalar.activation(out=sq[:], in_=live["acc", m, n][:], func=SQUARE)
+        def multiply(m, n, t_first=False, lo=0, hi=CHUNK):
+            acc = sums_pool.tile([P, CHUNK], F32, name="acc")
+            live["acc", m, n, lo] = acc
+            view = acc[:, : hi - lo]
+            if t_first:
+                passes_t(m, n, view, lo, hi, True, False)
+                passes_s(m, n, view, lo, hi, False, True)
+            else:
+                passes_s(m, n, view, lo, hi, True, False)
+                passes_t(m, n, view, lo, hi, False, True)
 
-        def weigh(m, n):
-            res = work.tile([P, CHUNK], F32, name="res")
-            cols = slice(CHUNK * n, CHUNK * (n + 1))
+        def square(m, n, lo=0, hi=CHUNK):
+            sq = work.tile([P, CHUNK], F32, name="sq")
+            live["sq", m, n, lo] = sq
+            nc.scalar.activation(out=sq[:, : hi - lo], in_=live["acc", m, n, lo][:, : hi - lo], func=SQUARE)
+
+        def weigh(m, n, lo=0, hi=CHUNK, part=None, queue=None):
+            res = outs.tile([P, CHUNK], F32, name="res")
+            cols = slice(CHUNK * n + lo, CHUNK * n + hi)
             nc.vector.scalar_tensor_tensor(
-                out=res[:],
-                in0=live["sq", m, n][:],
+                out=res[:, : hi - lo],
+                in0=live["sq", m, n, lo][:, : hi - lo],
                 scalar=1.0,
                 in1=trust_all[:, cols],
                 op0=MULT,
                 op1=MULT,
-                accum_out=parts[:, m, n : n + 1],
+                accum_out=parts[:, m, n : n + 1] if part is None else part,
             )
-            nc.sync.dma_start(out=o_view[:, m, cols], in_=res[:])
+            (queue or nc.sync).dma_start(out=o_view[:, m, cols], in_=res[:, : hi - lo])
+
+        def group(m, n):
+            multiply(m, n)
+            square(m, n)
+            weigh(m, n)
 
         with tc.manual_schedule():
-            nc.sync.dma_start(out=scale[:], in_=teacher_scale.rearrange("(p m) c -> p m c", m=TILES))
+            nc.scalar.dma_start(out=scale[:], in_=teacher_scale.rearrange("(p m) c -> p m c", m=TILES))
+            nc.scalar.dma_start(out=trust_row[0:1, :], in_=trust.rearrange("(o n) -> o n", o=1))
+            load_t(0)
             load_s(0)
             load_b(0)
-            load_t(0)
-            load_b(1)
             for q in range(4):
                 nc.sync.dma_start(
                     out=tb_scales[32 * q : 32 * q + 4, :, :].bitcast(I32),
                     in_=tbank_scales[:, 4 * q : 4 * q + 4, :].rearrange("g q n -> q g n").bitcast(I32),
                 )
             load_words(0)
-            nc.sync.dma_start(out=trust_row[0:1, :], in_=trust.rearrange("(o n) -> o n", o=1))
-            load_b(2)
+            load_t(1)
+            load_s(1)
+            load_b(1)
             load_words(1)
+            load_t(2)
+            load_s(2)
+            load_b(2)
             load_words(2)
-            for m in range(1, TILES):
+            for m in range(3, TILES):
                 load_t(m)
                 load_s(m)
 
+            trust_banks = []
+            for n in range(CHUNKS):
+                bank = sums_pool.tile([P, CHUNK], F32, name="acc")
+                trust_banks.append(bank)
+
+            def spread_trust(n):
+                cols = slice(CHUNK * n, CHUNK * (n + 1))
+                nc.tensor.matmul(trust_banks[n][:], ones[:], trust_row[:, cols], start=True, stop=True)
+
+            def take_trust(n):
+                cols = slice(CHUNK * n, CHUNK * (n + 1))
+                nc.scalar.copy(out=trust_all[:, cols], in_=trust_banks[n][:])
+
+            def stir(n):
+                for i in range(n):
+                    bank = turned.tile([P, CHUNK], F32, name="bank")
+                    nc.tensor.matmul(bank[:], warm[:, :P], warm[:], start=True, stop=True)
+
             nc.vector.tensor_scalar(out=neg[:], in0=scale[:], scalar1=-1.0, scalar2=None, op0=MULT)
-            perm_s(0)
+            stir(5)
+            spread_trust(0)
+            widen(0, 0, 16)
             turn_s(0)
             take_s(0)
-            for i in range(4):
-                turn_b(i)
-                take_b(i, i % 2 == 0)
-                if i == 1:
-                    quant_s(0)
-            widen(0, 0, 16)
-            quant_b(0)
+            turn_b(0)
+            take_b(0, True)
+            spread_trust(1)
+            turn_b(1)
+            take_b(1, True)
             turn_t(0)
-            take_t(0)
-            for i in range(4, 8):
-                turn_b(i)
-                take_b(i, i % 2 == 0)
-                if i == 5:
-                    quant_t(0)
-            mm_s(0, 0)
-            quant_b(1)
-            for i in range(8, 12):
-                turn_b(i)
-                take_b(i, i % 2 == 0)
-            mm_s(0, 1)
-            mm_t(0, 0)
-            quant_b(2)
-            for n in range(CHUNKS):
-                bank = turned.tile([P, CHUNK], F32, name="bank")
-                cols = slice(CHUNK * n, CHUNK * (n + 1))
-                nc.tensor.matmul(bank[:], ones[:], trust_row[:, cols], start=True, stop=True)
-                nc.scalar.copy(out=trust_all[:, cols], in_=bank[:])
-            perm_s(1)
+            take_t(0, 0)
+            take_t(0, 1, False)
+            quant_s(0)
+            turn_b(2)
+            take_b(2, True)
+            spread_trust(2)
+            turn_b(3)
+            quant_t(0)
+            take_b(3, True)
+            quant_b(0)
+            multiply(0, 0, True)
+            take_trust(0)
             widen(1, 0, 16)
-            square(0, 0)
-            weigh(0, 0)
-            mm_s(0, 2)
-            mm_t(0, 1)
-            square(0, 1)
-            weigh(0, 1)
             turn_s(1)
-            turn_t(1)
             take_s(1)
-            take_t(1)
-            perm_s(2)
+            turn_b(4)
+            take_b(4, True)
+            square(0, 0)
+            turn_b(5)
+            take_b(5, True)
             quant_s(1)
+            turn_t(1)
+            take_t(1, 0)
+            take_t(1, 1)
+            weigh(0, 0)
+            turn_b(6)
+            take_b(6, True)
+            turn_b(7)
+            take_b(7, True)
             quant_t(1)
-            mm_t(0, 2)
-            square(0, 2)
-            weigh(0, 2)
+            multiply(1, 0)
             widen(2, 0, 16)
-
-            for m in range(1, TILES):
+            quant_b(1)
+            take_trust(1)
+            turn_s(2)
+            turn_t(2)
+            take_s(2)
+            square(1, 0)
+            take_t(2, 0)
+            take_t(2, 1)
+            weigh(1, 0)
+            multiply(0, 1)
+            take_trust(2)
+            quant_s(2)
+            quant_t(2)
+            turn_b(8)
+            turn_b(9)
+            square(0, 1)
+            take_b(8, True)
+            take_b(9, True)
+            weigh(0, 1)
+            multiply(1, 1)
+            turn_b(10)
+            turn_b(11)
+            square(1, 1)
+            take_b(10, True)
+            take_b(11, True)
+            weigh(1, 1)
+            multiply(2, 0)
+            quant_b(2)
+            perm_s(3)
+            widen(3, 0, 16)
+            square(2, 0)
+            multiply(2, 1)
+            weigh(2, 0)
+            perm_s(4)
+            turn_s(3)
+            turn_t(3)
+            multiply(0, 2)
+            square(2, 1)
+            take_s(3)
+            take_t(3, 0)
+            take_t(3, 1)
+            weigh(2, 1)
+            widen(4, 0, 4)
+            multiply(1, 2)
+            square(0, 2)
+            quant_s(3)
+            quant_t(3)
+            weigh(0, 2)
+            multiply(2, 2)
+            square(1, 2)
+            widen(4, 4, 16)
+            weigh(1, 2)
+            pending = (2, 2)
+            for m in range(3, TILES):
                 ahead = m + 1 < TILES
                 further = m + 2 < TILES
                 if ahead:
                     turn_s(m + 1)
                     turn_t(m + 1)
+                multiply(m, 0)
+                square(*pending)
+                if ahead:
                     take_s(m + 1)
-                    take_t(m + 1)
+                    take_t(m + 1, 0)
+                    take_t(m + 1, 1)
+                if further:
+                    widen(m + 2, 0, 6)
+                weigh(*pending)
                 if further:
                     perm_s(m + 2)
                 if ahead:
                     quant_s(m + 1)
                     quant_t(m + 1)
-                for n in range(CHUNKS):
-                    mm_s(m, n)
-                    mm_t(m, n)
-                    square(m, n)
-                    if further and n < 2:
-                        widen(m + 2, 8 * n, 8 * n + 8)
-                    weigh(m, n)
-
+                multiply(m, 1)
+                square(m, 0)
+                if further:
+                    widen(m + 2, 6, 11)
+                weigh(m, 0)
+                if m < TILES - 1:
+                    multiply(m, 2)
+                square(m, 1)
+                if further:
+                    widen(m + 2, 11, 16)
+                weigh(m, 1)
+                pending = (m, 2)
+            last = TILES - 1
+            half = CHUNK // 2
+            quarter = CHUNK // 4
             total = const.tile([P, TILES], F32, name="total")
-            nc.vector.reduce_sum(out=total[:], in_=parts[:], axis=mybir.AxisListType.X)
-            nc.vector.tensor_scalar(out=means[:], in0=total[:], scalar1=1.0 / N, scalar2=None, op0=MULT)
-            nc.sync.dma_start(out=out_1.rearrange("(p m) -> p m", m=TILES), in_=means[:])
+            rest = const.tile([P, 1], F32, name="rest")
+            for h in range(2):
+                acc = sums_pool.tile([P, CHUNK], F32, name="acc")
+                live["acc", last, 2, half * h] = acc
+                for j in range(2):
+                    lo = half * h + quarter * j
+                    view = acc[:, quarter * j : quarter * (j + 1)]
+                    passes_s(last, 2, view, lo, lo + quarter, True, False)
+                    passes_t(last, 2, view, lo, lo + quarter, False, True)
+                square(last, 2, half * h, half * (h + 1))
+                if h == 0:
+                    weigh(last, 2, 0, half, part=parts[:, last, 2:3])
+                    nc.vector.reduce_sum(out=total[:], in_=parts[:], axis=mybir.AxisListType.X)
+                    nc.vector.tensor_scalar(out=means[:, :last], in0=total[:, :last], scalar1=1.0 / N, scalar2=None, op0=MULT)
+            weigh(last, 2, half, CHUNK, part=rest[:, 0:1])
+            nc.vector.tensor_scalar(
+                out=means[:, last:],
+                in0=total[:, last:],
+                scalar1=rest[:, 0:1],
+                scalar2=1.0 / N,
+                op0=mybir.AluOpType.add,
+                op1=MULT,
+            )
+            nc.scalar.dma_start(out=out_1.rearrange("(p m) -> p m", m=TILES), in_=means[:])

@@ -41,12 +41,12 @@ def tile_bank_relation_distill_d6_kernel(
         nc.gpsimd.memset(warm[:].bitcast(I32), 0)
         ones = const.tile([P, P], BF16, name="ones")
         trust_row = const.tile([P, N], BF16, name="trust_row")
-        nc.vector.memset(trust_row[:].bitcast(I32), 0)
+        nc.gpsimd.memset(trust_row[:].bitcast(I32), 0)
         nc.gpsimd.memset(ones[:], 1.0)
         ident = const.tile([P, P], F32, name="ident")
         make_identity(nc, ident[:])
         trust_all = const.tile([P, N], F32, name="trust_all")
-        tb_words = const.tile([P, GT, 2 * N], U8, name="tb_words", align_bytes=64)
+        tb_words = [const.tile([P, GT, 2 * CHUNK], U8, name="tb_words%d" % n, align_bytes=64) for n in range(CHUNKS)]
         tb_scales = const.tile([P, GT, N], U8, name="tb_scales", align_bytes=64)
         nc.vector.memset(tb_scales[:].rearrange("p g n -> p (g n)").bitcast(I32), 0)
         scale = const.tile([P, TILES, K // P], F32, name="scale")
@@ -77,7 +77,7 @@ def tile_bank_relation_distill_d6_kernel(
         def load_words(c):
             cols = slice(2 * CHUNK * c, 2 * CHUNK * (c + 1))
             nc.sync.dma_start(
-                out=tb_words[:, :, cols].bitcast(I32),
+                out=tb_words[c][:].bitcast(I32),
                 in_=tbank_words[:, :, cols].rearrange("g p w -> p g w").bitcast(I32),
             )
 
@@ -161,13 +161,24 @@ def tile_bank_relation_distill_d6_kernel(
                 in_=live["gt", m][:].rearrange("p g r u -> p (g r u)").bitcast(BF16),
             )
 
+        def perm_b(i):
+            xb = work.tile([P, GS, 2, P], F32, name="xb")
+            live["xb", i] = xb
+            nc.vector.tensor_copy(
+                out=xb[:], in_=b_raw[i][:].bitcast(F32).rearrange("p (g w u) -> p g u w", g=GS, u=2)
+            )
+
         def turn_b(i):
             bank = turned.tile([P, GS, 2, P], F32, name="bank")
             live["bb", i] = bank
             words = b_raw[i][:].bitcast(F32)
             for g in range(GS):
                 for u in range(2):
-                    nc.tensor.transpose(bank[:, g, u, :], words[:, 256 * g + u : 256 * (g + 1) : 2], ident[:])
+                    if ("xb", i) in live:
+                        rows = live["xb", i][:, g, u, :]
+                    else:
+                        rows = words[:, 256 * g + u : 256 * (g + 1) : 2]
+                    nc.tensor.transpose(bank[:, g, u, :], rows, ident[:])
 
         def take_b(i, on_scalar):
             c, j = divmod(i, 4)
@@ -208,7 +219,7 @@ def tile_bank_relation_distill_d6_kernel(
                     out=acc,
                     lhsT=codes[:, g, :].bitcast(FP8X4),
                     lhsT_scale=scales[:, g, :],
-                    rhs=tb_words[:, g, 2 * (CHUNK * n + lo) : 2 * (CHUNK * n + hi)].bitcast(FP4X4),
+                    rhs=tb_words[n][:, g, 2 * lo : 2 * hi].bitcast(FP4X4),
                     rhs_scale=tb_scales[:, g, CHUNK * n + lo : CHUNK * n + hi],
                     start=first and g == 0,
                     stop=last and g == GT - 1,
@@ -224,6 +235,14 @@ def tile_bank_relation_distill_d6_kernel(
             else:
                 passes_s(m, n, view, lo, hi, True, False)
                 passes_t(m, n, view, lo, hi, False, True)
+
+        def open_group(m, n):
+            acc = sums_pool.tile([P, CHUNK], F32, name="acc")
+            live["acc", m, n, 0] = acc
+            passes_t(m, n, acc[:], 0, CHUNK, True, False)
+
+        def close_group(m, n):
+            passes_s(m, n, live["acc", m, n, 0][:], 0, CHUNK, False, True)
 
         def square(m, n, lo=0, hi=CHUNK):
             sq = work.tile([P, CHUNK], F32, name="sq")
@@ -251,10 +270,10 @@ def tile_bank_relation_distill_d6_kernel(
 
         with tc.manual_schedule():
             nc.scalar.dma_start(out=scale[:], in_=teacher_scale.rearrange("(p m) c -> p m c", m=TILES))
-            nc.scalar.dma_start(out=trust_row[0:1, :], in_=trust.rearrange("(o n) -> o n", o=1))
             load_t(0)
             load_s(0)
             load_b(0)
+            nc.gpsimd.dma_start(out=trust_row[0:1, :], in_=trust.rearrange("(o n) -> o n", o=1))
             for q in range(4):
                 nc.sync.dma_start(
                     out=tb_scales[32 * q : 32 * q + 4, :, :].bitcast(I32),
@@ -292,16 +311,16 @@ def tile_bank_relation_distill_d6_kernel(
                     nc.tensor.matmul(bank[:], warm[:, :P], warm[:], start=True, stop=True)
 
             nc.vector.tensor_scalar(out=neg[:], in0=scale[:], scalar1=-1.0, scalar2=None, op0=MULT)
-            stir(5)
-            spread_trust(0)
+            stir(6)
             widen(0, 0, 16)
             turn_s(0)
             take_s(0)
             turn_b(0)
             take_b(0, True)
-            spread_trust(1)
+            spread_trust(0)
             turn_b(1)
             take_b(1, True)
+            spread_trust(1)
             turn_t(0)
             take_t(0, 0)
             take_t(0, 1, False)
@@ -312,27 +331,30 @@ def tile_bank_relation_distill_d6_kernel(
             turn_b(3)
             quant_t(0)
             take_b(3, True)
+            widen(1, 0, 8)
             quant_b(0)
-            multiply(0, 0, True)
-            take_trust(0)
-            widen(1, 0, 16)
+            widen(1, 8, 16)
+            open_group(0, 0)
             turn_s(1)
             take_s(1)
+            take_trust(0)
             turn_b(4)
             take_b(4, True)
-            square(0, 0)
-            turn_b(5)
-            take_b(5, True)
+            close_group(0, 0)
             quant_s(1)
             turn_t(1)
             take_t(1, 0)
             take_t(1, 1)
-            weigh(0, 0)
+            turn_b(5)
+            take_b(5, False)
+            square(0, 0)
             turn_b(6)
             take_b(6, True)
+            quant_t(1)
+            weigh(0, 0)
+            perm_s(2)
             turn_b(7)
             take_b(7, True)
-            quant_t(1)
             multiply(1, 0)
             widen(2, 0, 16)
             quant_b(1)
@@ -340,52 +362,58 @@ def tile_bank_relation_distill_d6_kernel(
             turn_s(2)
             turn_t(2)
             take_s(2)
+            take_trust(2)
             square(1, 0)
             take_t(2, 0)
             take_t(2, 1)
             weigh(1, 0)
-            multiply(0, 1)
-            take_trust(2)
+            multiply(0, 1, True)
             quant_s(2)
             quant_t(2)
+            perm_b(8)
+            square(0, 1)
+            multiply(1, 1)
+            perm_b(9)
+            weigh(0, 1)
             turn_b(8)
             turn_b(9)
-            square(0, 1)
+            perm_b(10)
             take_b(8, True)
             take_b(9, True)
-            weigh(0, 1)
-            multiply(1, 1)
+            square(1, 1)
+            multiply(2, 0)
+            perm_b(11)
+            perm_s(3)
+            widen(3, 0, 12)
+            weigh(1, 1)
+            widen(3, 12, 16)
             turn_b(10)
             turn_b(11)
-            square(1, 1)
             take_b(10, True)
             take_b(11, True)
-            weigh(1, 1)
-            multiply(2, 0)
-            quant_b(2)
-            perm_s(3)
-            widen(3, 0, 16)
             square(2, 0)
             multiply(2, 1)
             weigh(2, 0)
-            perm_s(4)
+            quant_b(2)
             turn_s(3)
             turn_t(3)
-            multiply(0, 2)
             square(2, 1)
             take_s(3)
             take_t(3, 0)
             take_t(3, 1)
+            multiply(0, 2, True)
             weigh(2, 1)
+            perm_s(4)
             widen(4, 0, 4)
-            multiply(1, 2)
-            square(0, 2)
             quant_s(3)
             quant_t(3)
+            square(0, 2)
+            multiply(1, 2)
+            widen(4, 4, 12)
             weigh(0, 2)
-            multiply(2, 2)
             square(1, 2)
-            widen(4, 4, 16)
+            multiply(2, 2)
+            widen(4, 12, 16)
             weigh(1, 2)
             pending = (2, 2)
             for m in range(3, TILES):

@@ -34,17 +34,18 @@ def tile_bank_relation_distill_d6_kernel(
         work = ctx.enter_context(tc.tile_pool(name="work", bufs=3))
         keep = ctx.enter_context(tc.tile_pool(name="keep", bufs=6))
         outs = ctx.enter_context(tc.tile_pool(name="outs", bufs=6))
+        wide = ctx.enter_context(tc.tile_pool(name="wide", bufs=4))
         turned = ctx.enter_context(tc.psum_pool(name="turned", bufs=4))
         sums_pool = ctx.enter_context(tc.psum_pool(name="acc", bufs=4))
 
         warm = const.tile([P, CHUNK], BF16, name="warm")
         nc.gpsimd.memset(warm[:].bitcast(I32), 0)
-        ones = const.tile([P, P], BF16, name="ones")
-        trust_row = const.tile([P, N], BF16, name="trust_row")
-        nc.gpsimd.memset(trust_row[:].bitcast(I32), 0)
-        nc.gpsimd.memset(ones[:], 1.0)
         ident = const.tile([P, P], F32, name="ident")
         make_identity(nc, ident[:])
+        ones = const.tile([P, P], BF16, name="ones")
+        trust_row = const.tile([P, N], BF16, name="trust_row")
+        nc.vector.memset(trust_row[:].bitcast(I32), 0)
+        nc.gpsimd.memset(ones[:], 1.0)
         trust_all = const.tile([P, N], F32, name="trust_all")
         tb_words = [const.tile([P, GT, 2 * CHUNK], U8, name="tb_words%d" % n, align_bytes=64) for n in range(CHUNKS)]
         tb_scales = const.tile([P, GT, N], U8, name="tb_scales", align_bytes=64)
@@ -162,7 +163,7 @@ def tile_bank_relation_distill_d6_kernel(
             )
 
         def perm_b(i):
-            xb = work.tile([P, GS, 2, P], F32, name="xb")
+            xb = wide.tile([P, GS, 2, P], F32, name="xb")
             live["xb", i] = xb
             nc.vector.tensor_copy(
                 out=xb[:], in_=b_raw[i][:].bitcast(F32).rearrange("p (g w u) -> p g u w", g=GS, u=2)
@@ -273,7 +274,7 @@ def tile_bank_relation_distill_d6_kernel(
             load_t(0)
             load_s(0)
             load_b(0)
-            nc.gpsimd.dma_start(out=trust_row[0:1, :], in_=trust.rearrange("(o n) -> o n", o=1))
+            nc.sync.dma_start(out=trust_row[0:1, :], in_=trust.rearrange("(o n) -> o n", o=1))
             for q in range(4):
                 nc.sync.dma_start(
                     out=tb_scales[32 * q : 32 * q + 4, :, :].bitcast(I32),
@@ -317,18 +318,18 @@ def tile_bank_relation_distill_d6_kernel(
             take_s(0)
             turn_b(0)
             take_b(0, True)
-            spread_trust(0)
             turn_b(1)
             take_b(1, True)
-            spread_trust(1)
             turn_t(0)
             take_t(0, 0)
             take_t(0, 1, False)
+            spread_trust(0)
             quant_s(0)
             turn_b(2)
             take_b(2, True)
-            spread_trust(2)
+            spread_trust(1)
             turn_b(3)
+            spread_trust(2)
             quant_t(0)
             take_b(3, True)
             widen(1, 0, 8)
@@ -342,6 +343,8 @@ def tile_bank_relation_distill_d6_kernel(
             take_b(4, True)
             close_group(0, 0)
             quant_s(1)
+            perm_b(6)
+            perm_b(7)
             turn_t(1)
             take_t(1, 0)
             take_t(1, 1)
@@ -372,29 +375,24 @@ def tile_bank_relation_distill_d6_kernel(
             quant_t(2)
             perm_b(8)
             square(0, 1)
-            multiply(1, 1)
             perm_b(9)
-            weigh(0, 1)
-            turn_b(8)
-            turn_b(9)
+            multiply(1, 1)
             perm_b(10)
-            take_b(8, True)
-            take_b(9, True)
-            square(1, 1)
-            multiply(2, 0)
+            weigh(0, 1)
             perm_b(11)
+            for i in range(8, 12):
+                turn_b(i)
+                take_b(i, True)
+            square(1, 1)
             perm_s(3)
-            widen(3, 0, 12)
+            widen(3, 0, 8)
+            multiply(2, 0)
             weigh(1, 1)
-            widen(3, 12, 16)
-            turn_b(10)
-            turn_b(11)
-            take_b(10, True)
-            take_b(11, True)
+            widen(3, 8, 16)
             square(2, 0)
+            quant_b(2)
             multiply(2, 1)
             weigh(2, 0)
-            quant_b(2)
             turn_s(3)
             turn_t(3)
             square(2, 1)

from contextlib import ExitStack

import concourse.mybir as mybir
from concourse.masks import make_identity

M, K, J, N = 1024, 2048, 1024, 1536
FLOPS = 2 * M * N * (K + J)

F32 = mybir.dt.float32
BF16 = mybir.dt.bfloat16
I32 = mybir.dt.int32
U32 = mybir.dt.uint32
U8 = mybir.dt.uint8
FP8 = mybir.dt.float8_e4m3fn
FP8X4 = mybir.dt.float8_e4m3fn_x4
FP4X4 = mybir.dt.float4_e2m1fn_x4
MULT = mybir.AluOpType.mult
SQUARE = mybir.ActivationFunctionType.Square

P = 128
TILES = M // P
CHUNK = 512
CHUNKS = N // CHUNK
GT = K // 512
GS = J // 512


def tile_bank_relation_distill_d6_kernel(
    tc, teacher_bytes, teacher_scale, tbank_words, tbank_scales, student, sbank, trust, out_0, out_1
):
    nc = tc.nc
    with ExitStack() as ctx:
        const = ctx.enter_context(tc.tile_pool(name="const", bufs=1))
        work = ctx.enter_context(tc.tile_pool(name="work", bufs=3))
        keep = ctx.enter_context(tc.tile_pool(name="keep", bufs=6))
        outs = ctx.enter_context(tc.tile_pool(name="outs", bufs=6))
        wide = ctx.enter_context(tc.tile_pool(name="wide", bufs=4))
        turned = ctx.enter_context(tc.psum_pool(name="turned", bufs=4))
        sums_pool = ctx.enter_context(tc.psum_pool(name="acc", bufs=4))

        warm = const.tile([P, CHUNK], BF16, name="warm")
        nc.gpsimd.memset(warm[:].bitcast(I32), 0)
        ident = const.tile([P, P], F32, name="ident")
        make_identity(nc, ident[:])
        ones = const.tile([P, P], BF16, name="ones")
        trust_row = const.tile([P, N], BF16, name="trust_row")
        nc.vector.memset(trust_row[:].bitcast(I32), 0)
        nc.gpsimd.memset(ones[:], 1.0)
        trust_all = const.tile([P, N], F32, name="trust_all")
        tb_words = [const.tile([P, GT, 2 * CHUNK], U8, name="tb_words%d" % n, align_bytes=64) for n in range(CHUNKS)]
        tb_scales = const.tile([P, GT, N], U8, name="tb_scales", align_bytes=64)
        nc.vector.memset(tb_scales[:].rearrange("p g n -> p (g n)").bitcast(I32), 0)
        scale = const.tile([P, TILES, K // P], F32, name="scale")
        neg = const.tile([P, TILES, K // P], F32, name="neg")
        parts = const.tile([P, TILES, CHUNKS], F32, name="parts")
        means = const.tile([P, TILES], F32, name="means")

        t_view = teacher_bytes.rearrange("(p m) k -> p m k", m=TILES)
        s_view = student.rearrange("(p m) k -> p m k", m=TILES)
        o_view = out_0.rearrange("(p m) n -> p m n", m=TILES)

        t_raw = [const.tile([P, K], U8, name="t_raw%d" % m, align_bytes=64) for m in range(TILES)]
        s_raw = [const.tile([P, J], BF16, name="s_raw%d" % m, align_bytes=64) for m in range(TILES)]
        b_raw = [const.tile([P, J], BF16, name="b_raw%d" % i, align_bytes=64) for i in range(N // P)]
        b_codes = const.tile([P, CHUNKS, GS, CHUNK], U32, name="b_codes", align_bytes=64)
        b_scales = const.tile([P, CHUNKS, GS, CHUNK], U8, name="b_scales", align_bytes=64)

        def load_s(m):
            nc.sync.dma_start(out=s_raw[m][:], in_=s_view[:, m, :])

        def load_t(m):
            nc.sync.dma_start(out=t_raw[m][:], in_=t_view[:, m, :])

        def load_b(c):
            for i in range(4 * c, 4 * c + 4):
                nc.sync.dma_start(out=b_raw[i][:], in_=sbank[P * i : P * (i + 1), :])

        def load_words(c):
            cols = slice(2 * CHUNK * c, 2 * CHUNK * (c + 1))
            nc.sync.dma_start(
                out=tb_words[c][:].bitcast(I32),
                in_=tbank_words[:, :, cols].rearrange("g p w -> p g w").bitcast(I32),
            )

        live = {}

        def perm_s(m):
            xs = work.tile([P, GS, 2, P], F32, name="xs")
            live["xs", m] = xs
            nc.vector.tensor_copy(
                out=xs[:], in_=s_raw[m][:].bitcast(F32).rearrange("p (g w u) -> p g u w", g=GS, u=2)
            )

        def turn_s(m):
            bank = turned.tile([P, GS, 2, P], F32, name="bank")
            live["bs", m] = bank
            words = s_raw[m][:].bitcast(F32)
            for g in range(GS):
                for u in range(2):
                    if ("xs", m) in live:
                        rows = live["xs", m][:, g, u, :]
                    else:
                        rows = words[:, 256 * g + u : 256 * (g + 1) : 2]
                    nc.tensor.transpose(bank[:, g, u, :], rows, ident[:])

        def take_s(m):
            grouped = work.tile([P, GS, P, 2], F32, name="s_grouped", align_bytes=64)
            live["gs", m] = grouped
            nc.scalar.copy(out=grouped[:], in_=live["bs", m][:].rearrange("p g u r -> p g r u"))

        def quant_s(m):
            codes = keep.tile([P, GS, P], U32, name="s_codes", align_bytes=64)
            scales = keep.tile([P, GS, P], U8, name="s_scales", align_bytes=64)
            live["cs", m] = (codes, scales)
            nc.vector.quantize_mx(
                out=codes[:].rearrange("p g r -> p (g r)").bitcast(FP8X4),
                scales=scales[:].rearrange("p g r -> p (g r)"),
                in_=live["gs", m][:].rearrange("p g r u -> p (g r u)").bitcast(BF16),
            )

        def widen(m, lo, hi):
            if lo == 0:
                live["xt", m] = work.tile([P, GT, 2, P, 2], BF16, name="xt", align_bytes=64)
            xt = live["xt", m]
            for c in range(lo, hi):
                g, q = divmod(c, 4)
                nc.vector.tensor_scalar(
                    out=xt[:, g, :, 32 * q : 32 * (q + 1), :].rearrange("p u w e -> p w u e"),
                    in0=t_raw[m][:, P * c : P * (c + 1)].bitcast(FP8).rearrange("p (w u e) -> p w u e", u=2, e=2),
                    scalar1=neg[:, m, c : c + 1],
                    scalar2=None,
                    op0=MULT,
                )

        def turn_t(m):
            words = live["xt", m][:].rearrange("p g u w e -> p (g u w e)").bitcast(F32)
            for h in range(2):
                bank = turned.tile([P, 2, 2, P], F32, name="bank")
                live["bt", m, h] = bank
                for g in range(2):
                    for u in range(2):
                        at = P * (2 * (2 * h + g) + u)
                        nc.tensor.transpose(bank[:, g, u, :], words[:, at : at + P], ident[:])

        def take_t(m, h, on_scalar=True):
            if h == 0:
                live["gt", m] = work.tile([P, GT, P, 2], F32, name="t_grouped", align_bytes=64)
            dst = live["gt", m][:, 2 * h : 2 * h + 2]
            src = live["bt", m, h][:].rearrange("p g u r -> p g r u")
            if on_scalar:
                nc.scalar.copy(out=dst, in_=src)
            else:
                nc.vector.tensor_copy(out=dst, in_=src)

        def quant_t(m):
            codes = keep.tile([P, GT, P], U32, name="t_codes", align_bytes=64)
            scales = keep.tile([P, GT, P], U8, name="t_scales", align_bytes=64)
            live["ct", m] = (codes, scales)
            nc.vector.quantize_mx(
                out=codes[:].rearrange("p g r -> p (g r)").bitcast(FP8X4),
                scales=scales[:].rearrange("p g r -> p (g r)"),
                in_=live["gt", m][:].rearrange("p g r u -> p (g r u)").bitcast(BF16),
            )

        def perm_b(i):
            xb = wide.tile([P, GS, 2, P], F32, name="xb")
            live["xb", i] = xb
            nc.vector.tensor_copy(
                out=xb[:], in_=b_raw[i][:].bitcast(F32).rearrange("p (g w u) -> p g u w", g=GS, u=2)
            )

        def turn_b(i):
            bank = turned.tile([P, GS, 2, P], F32, name="bank")
            live["bb", i] = bank
            words = b_raw[i][:].bitcast(F32)
            for g in range(GS):
                for u in range(2):
                    if ("xb", i) in live:
                        rows = live["xb", i][:, g, u, :]
                    else:
                        rows = words[:, 256 * g + u : 256 * (g + 1) : 2]
                    nc.tensor.transpose(bank[:, g, u, :], rows, ident[:])

        def take_b(i, on_scalar):
            c, j = divmod(i, 4)
            if j == 0:
                live["gb", c] = work.tile([P, GS, CHUNK, 2], F32, name="b_grouped", align_bytes=64)
            dst = live["gb", c][:, :, P * j : P * (j + 1), :]
            src = live["bb", i][:].rearrange("p g u r -> p g r u")
            if on_scalar:
                nc.scalar.copy(out=dst, in_=src)
            else:
                nc.vector.tensor_copy(out=dst, in_=src)

        def quant_b(c):
            for g in range(GS):
                nc.vector.quantize_mx(
                    out=b_codes[:, c, g, :].bitcast(FP8X4),
                    scales=b_scales[:, c, g, :],
                    in_=live["gb", c][:, g].rearrange("p r u -> p (r u)").bitcast(BF16),
                )

        def passes_s(m, n, acc, lo, hi, first, last):
            codes, scales = live["cs", m]
            for g in range(GS):
                nc.tensor.matmul_mx(
                    out=acc,
                    lhsT=codes[:, g, :].bitcast(FP8X4),
                    lhsT_scale=scales[:, g, :],
                    rhs=b_codes[:, n, g, lo:hi].bitcast(FP8X4),
                    rhs_scale=b_scales[:, n, g, lo:hi],
                    start=first and g == 0,
                    stop=last and g == GS - 1,
                )

        def passes_t(m, n, acc, lo, hi, first, last):
            codes, scales = live["ct", m]
            for g in range(GT):
                nc.tensor.matmul_mx(
                    out=acc,
                    lhsT=codes[:, g, :].bitcast(FP8X4),
                    lhsT_scale=scales[:, g, :],
                    rhs=tb_words[n][:, g, 2 * lo : 2 * hi].bitcast(FP4X4),
                    rhs_scale=tb_scales[:, g, CHUNK * n + lo : CHUNK * n + hi],
                    start=first and g == 0,
                    stop=last and g == GT - 1,
                )

        def multiply(m, n, t_first=False, lo=0, hi=CHUNK):
            acc = sums_pool.tile([P, CHUNK], F32, name="acc")
            live["acc", m, n, lo] = acc
            view = acc[:, : hi - lo]
            if t_first:
                passes_t(m, n, view, lo, hi, True, False)
                passes_s(m, n, view, lo, hi, False, True)
            else:
                passes_s(m, n, view, lo, hi, True, False)
                passes_t(m, n, view, lo, hi, False, True)

        def open_group(m, n):
            acc = sums_pool.tile([P, CHUNK], F32, name="acc")
            live["acc", m, n, 0] = acc
            passes_t(m, n, acc[:], 0, CHUNK, True, False)

        def close_group(m, n):
            passes_s(m, n, live["acc", m, n, 0][:], 0, CHUNK, False, True)

        def square(m, n, lo=0, hi=CHUNK):
            sq = work.tile([P, CHUNK], F32, name="sq")
            live["sq", m, n, lo] = sq
            nc.scalar.activation(out=sq[:, : hi - lo], in_=live["acc", m, n, lo][:, : hi - lo], func=SQUARE)

        def weigh(m, n, lo=0, hi=CHUNK, part=None, queue=None):
            res = outs.tile([P, CHUNK], F32, name="res")
            cols = slice(CHUNK * n + lo, CHUNK * n + hi)
            nc.vector.scalar_tensor_tensor(
                out=res[:, : hi - lo],
                in0=live["sq", m, n, lo][:, : hi - lo],
                scalar=1.0,
                in1=trust_all[:, cols],
                op0=MULT,
                op1=MULT,
                accum_out=parts[:, m, n : n + 1] if part is None else part,
            )
            (queue or nc.sync).dma_start(out=o_view[:, m, cols], in_=res[:, : hi - lo])

        def group(m, n):
            multiply(m, n)
            square(m, n)
            weigh(m, n)

        with tc.manual_schedule():
            nc.scalar.dma_start(out=scale[:], in_=teacher_scale.rearrange("(p m) c -> p m c", m=TILES))
            load_t(0)
            load_s(0)
            load_b(0)
            nc.sync.dma_start(out=trust_row[0:1, :], in_=trust.rearrange("(o n) -> o n", o=1))
            for q in range(4):
                nc.sync.dma_start(
                    out=tb_scales[32 * q : 32 * q + 4, :, :].bitcast(I32),
                    in_=tbank_scales[:, 4 * q : 4 * q + 4, :].rearrange("g q n -> q g n").bitcast(I32),
                )
            load_words(0)
            load_t(1)
            load_s(1)
            load_b(1)
            load_words(1)
            load_t(2)
            load_s(2)
            load_b(2)
            load_words(2)
            for m in range(3, TILES):
                load_t(m)
                load_s(m)

            trust_banks = []
            for n in range(CHUNKS):
                bank = sums_pool.tile([P, CHUNK], F32, name="acc")
                trust_banks.append(bank)

            def spread_trust(n):
                cols = slice(CHUNK * n, CHUNK * (n + 1))
                nc.tensor.matmul(trust_banks[n][:], ones[:], trust_row[:, cols], start=True, stop=True)

            def take_trust(n):
                cols = slice(CHUNK * n, CHUNK * (n + 1))
                nc.scalar.copy(out=trust_all[:, cols], in_=trust_banks[n][:])

            def stir(n):
                for i in range(n):
                    bank = turned.tile([P, CHUNK], F32, name="bank")
                    nc.tensor.matmul(bank[:], warm[:, :P], warm[:], start=True, stop=True)

            nc.vector.tensor_scalar(out=neg[:], in0=scale[:], scalar1=-1.0, scalar2=None, op0=MULT)
            stir(6)
            widen(0, 0, 16)
            turn_s(0)
            take_s(0)
            turn_b(0)
            take_b(0, True)
            turn_b(1)
            take_b(1, True)
            turn_t(0)
            take_t(0, 0)
            take_t(0, 1, False)
            spread_trust(0)
            quant_s(0)
            turn_b(2)
            take_b(2, True)
            spread_trust(1)
            turn_b(3)
            spread_trust(2)
            quant_t(0)
            take_b(3, True)
            widen(1, 0, 8)
            quant_b(0)
            widen(1, 8, 16)
            open_group(0, 0)
            turn_s(1)
            take_s(1)
            take_trust(0)
            turn_b(4)
            take_b(4, True)
            close_group(0, 0)
            quant_s(1)
            perm_b(6)
            perm_b(7)
            turn_t(1)
            take_t(1, 0)
            take_t(1, 1)
            turn_b(5)
            take_b(5, False)
            square(0, 0)
            turn_b(6)
            take_b(6, True)
            quant_t(1)
            weigh(0, 0)
            perm_s(2)
            turn_b(7)
            take_b(7, True)
            multiply(1, 0)
            widen(2, 0, 16)
            quant_b(1)
            take_trust(1)
            turn_s(2)
            turn_t(2)
            take_s(2)
            take_trust(2)
            square(1, 0)
            take_t(2, 0)
            take_t(2, 1)
            weigh(1, 0)
            multiply(0, 1, True)
            quant_s(2)
            quant_t(2)
            perm_b(8)
            square(0, 1)
            perm_b(9)
            multiply(1, 1)
            perm_b(10)
            weigh(0, 1)
            perm_b(11)
            for i in range(8, 12):
                turn_b(i)
                take_b(i, True)
            square(1, 1)
            perm_s(3)
            widen(3, 0, 8)
            multiply(2, 0)
            weigh(1, 1)
            widen(3, 8, 16)
            square(2, 0)
            quant_b(2)
            multiply(2, 1)
            weigh(2, 0)
            turn_s(3)
            turn_t(3)
            square(2, 1)
            take_s(3)
            take_t(3, 0)
            take_t(3, 1)
            multiply(0, 2, True)
            weigh(2, 1)
            perm_s(4)
            widen(4, 0, 4)
            quant_s(3)
            quant_t(3)
            square(0, 2)
            multiply(1, 2)
            widen(4, 4, 12)
            weigh(0, 2)
            square(1, 2)
            multiply(2, 2)
            widen(4, 12, 16)
            weigh(1, 2)
            pending = (2, 2)
            for m in range(3, TILES):
                ahead = m + 1 < TILES
                further = m + 2 < TILES
                if ahead:
                    turn_s(m + 1)
                    turn_t(m + 1)
                multiply(m, 0)
                square(*pending)
                if ahead:
                    take_s(m + 1)
                    take_t(m + 1, 0)
                    take_t(m + 1, 1)
                if further:
                    widen(m + 2, 0, 6)
                weigh(*pending)
                if further:
                    perm_s(m + 2)
                if ahead:
                    quant_s(m + 1)
                    quant_t(m + 1)
                multiply(m, 1)
                square(m, 0)
                if further:
                    widen(m + 2, 6, 11)
                weigh(m, 0)
                if m < TILES - 1:
                    multiply(m, 2)
                square(m, 1)
                if further:
                    widen(m + 2, 11, 16)
                weigh(m, 1)
                pending = (m, 2)
            last = TILES - 1
            half = CHUNK // 2
            quarter = CHUNK // 4
            total = const.tile([P, TILES], F32, name="total")
            rest = const.tile([P, 1], F32, name="rest")
            for h in range(2):
                acc = sums_pool.tile([P, CHUNK], F32, name="acc")
                live["acc", last, 2, half * h] = acc
                for j in range(2):
                    lo = half * h + quarter * j
                    view = acc[:, quarter * j : quarter * (j + 1)]
                    passes_s(last, 2, view, lo, lo + quarter, True, False)
                    passes_t(last, 2, view, lo, lo + quarter, False, True)
                square(last, 2, half * h, half * (h + 1))
                if h == 0:
                    weigh(last, 2, 0, half, part=parts[:, last, 2:3])
                    nc.vector.reduce_sum(out=total[:], in_=parts[:], axis=mybir.AxisListType.X)
                    nc.vector.tensor_scalar(out=means[:, :last], in0=total[:, :last], scalar1=1.0 / N, scalar2=None, op0=MULT)
            weigh(last, 2, half, CHUNK, part=rest[:, 0:1])
            nc.vector.tensor_scalar(
                out=means[:, last:],
                in0=total[:, last:],
                scalar1=rest[:, 0:1],
                scalar2=1.0 / N,
                op0=mybir.AluOpType.add,
                op1=MULT,
            )
            nc.scalar.dma_start(out=out_1.rearrange("(p m) -> p m", m=TILES), in_=means[:])
